import numpy as np
import ml_dtypes

BF16 = ml_dtypes.bfloat16


def bf(x):
    return np.asarray(x, np.float32).astype(BF16)


def f32(x):
    return np.asarray(x, np.float32)


def f64(x):
    return np.asarray(x).astype(np.float64)


def striped(idx):
    return np.concatenate([l.reshape(-1, 16).T for l in idx])


def rows(idx, k):
    return np.tile(np.repeat(idx, 16, axis=0), (k // (16 * 8), 1))


def look(tab, idx):
    return np.take_along_axis(f64(tab), rows(idx, len(tab)), axis=1)


K, S, V, N = 256, 2048, 1536, 1536


def setup_inputs():
    return {"tab": f32(np.random.standard_normal((2, K, S))), "y": f32(np.random.standard_normal((K, V))), "offs": striped(np.stack([np.random.permutation(S)[:N] for _ in range(8)]))}


def reference(tab, y, offs):
    idx = np.stack([g.T.reshape(-1) for g in np.split(offs, 8)])
    x = (look(tab[0], idx) + f64(y)) * (np.tanh(look(tab[1], idx)))
    return x

@@ -1,0 +1,44 @@
+import concourse.mybir as mybir
+
+F32 = mybir.dt.float32
+U16 = mybir.dt.uint16
+ADD = mybir.AluOpType.add
+MULT = mybir.AluOpType.mult
+TANH = mybir.ActivationFunctionType.Tanh
+
+P = 128
+PIECE = 512
+PER_COLUMN = 16
+
+
+def tile_lookup_vg_addtanh_out_kernel(tc, tab, y, offs, out):
+    nc = tc.nc
+    rows, places = tab.shape[1], tab.shape[2]
+    n = y.shape[1]
+    blocks = rows // P
+    pieces = n // PIECE
+    piece_columns = PIECE // PER_COLUMN
+
+    with tc.tile_pool(name="held", bufs=1) as held:
+        lists = held.tile([P, n // PER_COLUMN], U16, name="lists")
+        nc.sync.dma_start(lists[:], offs)
+
+        for b in range(blocks):
+            row = slice(b * P, (b + 1) * P)
+            gates = held.tile([P, places], F32, name="gates%d" % b)
+            values = held.tile([P, places], F32, name="values%d" % b)
+            stream = held.tile([P, n], F32, name="stream%d" % b)
+            nc.sync.dma_start(gates[:], tab[1, row, :])
+            nc.sync.dma_start(values[:], tab[0, row, :])
+            nc.sync.dma_start(stream[:], y[row, :])
+
+            gated = held.tile([P, n], F32, name="gated%d" % b)
+            summed = held.tile([P, n], F32, name="summed%d" % b)
+            result = held.tile([P, n], F32, name="result%d" % b)
+            for c in range(pieces):
+                col = slice(c * PIECE, (c + 1) * PIECE)
+                entries = lists[:, c * piece_columns:(c + 1) * piece_columns]
+                nc.scalar.activation(gated[:, col], gates[:].indirect(entries), TANH)
+                nc.vector.tensor_tensor(summed[:, col], values[:].indirect(entries), stream[:, col], ADD)
+                nc.vector.tensor_tensor(result[:, col], summed[:, col], gated[:, col], MULT)
+                nc.sync.dma_start(out[row, col], result[:, col])

@@ -23,22 +23,30 @@ def tile_lookup_vg_addtanh_out_kernel(tc, tab, y, offs, out):
         lists = held.tile([P, n // PER_COLUMN], U16, name="lists")
         nc.sync.dma_start(lists[:], offs)
 
+        values, streams, gates = [], [], []
         for b in range(blocks):
             row = slice(b * P, (b + 1) * P)
-            gates = held.tile([P, places], F32, name="gates%d" % b)
-            values = held.tile([P, places], F32, name="values%d" % b)
-            stream = held.tile([P, n], F32, name="stream%d" % b)
-            nc.sync.dma_start(gates[:], tab[1, row, :])
-            nc.sync.dma_start(values[:], tab[0, row, :])
-            nc.sync.dma_start(stream[:], y[row, :])
+            values.append(held.tile([P, places], F32, name="values%d" % b))
+            streams.append(held.tile([P, n], F32, name="stream%d" % b))
+            gates.append(held.tile([P, places], F32, name="gates%d" % b))
+            nc.sync.dma_start(values[b][:], tab[0, row, :])
+            nc.sync.dma_start(streams[b][:, :PIECE], y[row, :PIECE])
+            nc.sync.dma_start(gates[b][:], tab[1, row, :])
+            for c in range(1, pieces):
+                col = slice(c * PIECE, (c + 1) * PIECE)
+                nc.sync.dma_start(streams[b][:, col], y[row, col])
 
+        for b in range(blocks):
+            row = slice(b * P, (b + 1) * P)
             gated = held.tile([P, n], F32, name="gated%d" % b)
             summed = held.tile([P, n], F32, name="summed%d" % b)
             result = held.tile([P, n], F32, name="result%d" % b)
             for c in range(pieces):
                 col = slice(c * PIECE, (c + 1) * PIECE)
                 entries = lists[:, c * piece_columns:(c + 1) * piece_columns]
-                nc.scalar.activation(gated[:, col], gates[:].indirect(entries), TANH)
-                nc.vector.tensor_tensor(summed[:, col], values[:].indirect(entries), stream[:, col], ADD)
+                nc.scalar.activation(gated[:, col], gates[b][:].indirect(entries), TANH)
+                nc.vector.tensor_tensor(summed[:, col], values[b][:].indirect(entries), streams[b][:, col], ADD)
+            for c in range(pieces):
+                col = slice(c * PIECE, (c + 1) * PIECE)
                 nc.vector.tensor_tensor(result[:, col], summed[:, col], gated[:, col], MULT)
                 nc.sync.dma_start(out[row, col], result[:, col])

@@ -23,6 +23,11 @@ def tile_lookup_vg_addtanh_out_kernel(tc, tab, y, offs, out):
         lists = held.tile([P, n // PER_COLUMN], U16, name="lists")
         nc.sync.dma_start(lists[:], offs)
 
+        zeros = held.tile([P, 8], F32, name="zeros")
+        warmed = held.tile([P, 8], F32, name="warmed")
+        nc.vector.memset(zeros[:], 0.0)
+        nc.scalar.activation(warmed[:], zeros[:], TANH)
+
         values, streams, gates = [], [], []
         for b in range(blocks):
             row = slice(b * P, (b + 1) * P)

@@ -52,6 +52,9 @@ def tile_lookup_vg_addtanh_out_kernel(tc, tab, y, offs, out):
                 nc.scalar.activation(gated[:, col], gates[b][:].indirect(entries), TANH)
                 nc.vector.tensor_tensor(summed[:, col], values[b][:].indirect(entries), streams[b][:, col], ADD)
             for c in range(pieces):
-                col = slice(c * PIECE, (c + 1) * PIECE)
-                nc.vector.tensor_tensor(result[:, col], summed[:, col], gated[:, col], MULT)
-                nc.sync.dma_start(out[row, col], result[:, col])
+                is_last = b == blocks - 1 and c == pieces - 1
+                width = PIECE // 2 if is_last else PIECE
+                for start in range(c * PIECE, (c + 1) * PIECE, width):
+                    col = slice(start, start + width)
+                    nc.vector.tensor_tensor(result[:, col], summed[:, col], gated[:, col], MULT)
+                    nc.sync.dma_start(out[row, col], result[:, col])

import concourse.mybir as mybir

F32 = mybir.dt.float32
U16 = mybir.dt.uint16
ADD = mybir.AluOpType.add
MULT = mybir.AluOpType.mult
TANH = mybir.ActivationFunctionType.Tanh

P = 128
PIECE = 512
PER_COLUMN = 16


def tile_lookup_vg_addtanh_out_kernel(tc, tab, y, offs, out):
    nc = tc.nc
    rows, places = tab.shape[1], tab.shape[2]
    n = y.shape[1]
    blocks = rows // P
    pieces = n // PIECE
    piece_columns = PIECE // PER_COLUMN

    with tc.tile_pool(name="held", bufs=1) as held:
        lists = held.tile([P, n // PER_COLUMN], U16, name="lists")
        nc.sync.dma_start(lists[:], offs)

        zeros = held.tile([P, 8], F32, name="zeros")
        warmed = held.tile([P, 8], F32, name="warmed")
        nc.vector.memset(zeros[:], 0.0)
        nc.scalar.activation(warmed[:], zeros[:], TANH)

        values, streams, gates = [], [], []
        for b in range(blocks):
            row = slice(b * P, (b + 1) * P)
            values.append(held.tile([P, places], F32, name="values%d" % b))
            streams.append(held.tile([P, n], F32, name="stream%d" % b))
            gates.append(held.tile([P, places], F32, name="gates%d" % b))
            nc.sync.dma_start(values[b][:], tab[0, row, :])
            nc.sync.dma_start(streams[b][:, :PIECE], y[row, :PIECE])
            nc.sync.dma_start(gates[b][:], tab[1, row, :])
            for c in range(1, pieces):
                col = slice(c * PIECE, (c + 1) * PIECE)
                nc.sync.dma_start(streams[b][:, col], y[row, col])

        for b in range(blocks):
            row = slice(b * P, (b + 1) * P)
            gated = held.tile([P, n], F32, name="gated%d" % b)
            summed = held.tile([P, n], F32, name="summed%d" % b)
            result = held.tile([P, n], F32, name="result%d" % b)
            for c in range(pieces):
                col = slice(c * PIECE, (c + 1) * PIECE)
                entries = lists[:, c * piece_columns:(c + 1) * piece_columns]
                nc.scalar.activation(gated[:, col], gates[b][:].indirect(entries), TANH)
                nc.vector.tensor_tensor(summed[:, col], values[b][:].indirect(entries), streams[b][:, col], ADD)
            for c in range(pieces):
                is_last = b == blocks - 1 and c == pieces - 1
                width = PIECE // 2 if is_last else PIECE
                for start in range(c * PIECE, (c + 1) * PIECE, width):
                    col = slice(start, start + width)
                    nc.vector.tensor_tensor(result[:, col], summed[:, col], gated[:, col], MULT)
                    nc.sync.dma_start(out[row, col], result[:, col])
